import numpy as np
import ml_dtypes


def mxq(x, axis, fmt="e4m3"):
    dtype, down = {"e4m3": (ml_dtypes.float8_e4m3fn, 7), "e5m2": (ml_dtypes.float8_e5m2, 14)}[fmt]
    v = np.moveaxis(np.asarray(x, np.float32).astype(ml_dtypes.bfloat16).astype(np.float64), axis, -1)
    blocks = v.reshape(v.shape[:-1] + (-1, 32))
    amax = np.abs(blocks).max(-1, keepdims=True)
    byte = np.maximum(np.where(amax > 0, np.frexp(amax)[1] - 1 + 127, 0) - down, 1)
    scale = np.exp2(byte - 127.0)
    codes = (blocks / scale).astype(np.float32).astype(dtype).astype(np.float64)
    return np.moveaxis((codes * scale).reshape(v.shape), -1, axis)


WIDE = False


def mx_kscale(k):
    if not WIDE:
        return np.ones(k)
    levels = np.array([10, -10, 5, -5, 0])
    if k % 512:
        return np.exp2(np.random.permutation(np.resize(levels, k // 32))).repeat(32)
    a = np.empty((k // 512, 16))
    for p in range(k // 512):
        a[p, :8] = np.random.permutation(np.resize(levels, 8))
        for g in range(8):
            far = levels[np.abs(levels - a[p, g]) >= 10]
            a[p, g + 8] = far[np.random.randint(len(far))]
    return np.exp2(a.ravel()).repeat(32)


def f64(x):
    return np.asarray(x).astype(np.float64)


def striped(idx):
    return np.tile(idx.reshape(-1, 16).T, (8, 1)).astype(np.uint16)


def unstriped(offs):
    return offs[:16].T.reshape(-1).astype(np.int64)


def pack_weight(w):
    k, n = w.shape
    w = f64(np.asarray(w, np.float32).astype(ml_dtypes.bfloat16)).reshape(k // 32, 32, n)
    amax = np.abs(w).max(1)
    byte = np.clip(np.where(amax > 0, np.frexp(amax)[1] - 1 + 127 - 7, 1), 1, 254)
    scaled = (w * np.exp2(127.0 - byte)[:, None, :]).reshape(k, n).astype(np.float32)
    words = np.ascontiguousarray(scaled.reshape(k // 512, 128, 4, n).transpose(0, 1, 3, 2)).astype(ml_dtypes.float8_e4m3fn).view(np.uint8)
    return words, np.ascontiguousarray(byte.astype(np.uint8).reshape(k // 512, 16, n))


def unpack_weight(words, scales):
    g, p, n, _ = words.shape
    vals = np.ascontiguousarray(words).view(ml_dtypes.float8_e4m3fn).astype(np.float64) * np.repeat(np.exp2(scales.astype(np.float64) - 127.0), 8, axis=1)[..., None]
    return vals.transpose(0, 1, 3, 2).reshape(g * 512, n)


def relu(v):
    return np.maximum(v, 0.0)


K, T, S, V, H, N = 1024, 2048, 768, 256, 512, 128


def setup_inputs():
    n = np.random.standard_normal
    s = mx_kscale(K)[:, None]
    u = mx_kscale(H)
    packed_w4 = pack_weight(n((H, N)) / np.sqrt(H) / u[:, None])
    return {
        "xT": (n((K, T)) * s).astype(np.float32),
        "w1": (n((K, H)) / np.sqrt(K) / s * u).astype(np.float32),
        "w2": (n((K, H)) / np.sqrt(K) / s).astype(np.float32),
        "w3": (n((K, H)) / np.sqrt(K) / s).astype(np.float32),
        "w4_words": packed_w4[0],
        "w4_scales": packed_w4[1],
        "offs": striped(np.random.permutation(T)[:S]),
    }


def reference(xT, w1, w2, w3, w4_words, w4_scales, offs):
    xq = mxq(f64(xT)[:, unstriped(offs)], 0, "e4m3")
    z = (((mxq(f64(w1), 0, "e4m3").T @ xq[:, :V])) * ((mxq(f64(w2), 0, "e4m3").T @ xq[:, V:2 * V]))) * ((mxq(f64(w3), 0, "e4m3").T @ xq[:, 2 * V:3 * V]))
    return relu(unpack_weight(w4_words, w4_scales).T @ mxq(z, 0, "e4m3"))

@@ -1,0 +1,205 @@
+from contextlib import ExitStack
+
+import concourse.mybir as mybir
+
+K, T, V, H, N = 1024, 2048, 256, 512, 128
+PIECES = 3
+FLOPS = 2 * PIECES * K * H * V + 2 * H * N * V
+
+F32 = mybir.dt.float32
+BF16 = mybir.dt.bfloat16
+I32 = mybir.dt.int32
+U32 = mybir.dt.uint32
+U16 = mybir.dt.uint16
+U8 = mybir.dt.uint8
+FP8X4 = mybir.dt.float8_e4m3fn_x4
+MULT = mybir.AluOpType.mult
+
+P = 128
+PACK = 4
+K_PASS = P * PACK
+PASSES = K // K_PASS
+HALF = 128
+HALVES = V // HALF
+LIST_COLS = V // 16
+SHARES = {(0, 0): 0, (0, 1): 64, (1, 0): 72, (1, 1): 48, (2, 0): 56}
+LAST_SHARES = (76, 44)
+
+
+def tile_picked_trilin_relu_e_kernel(
+    tc, xT, w1, w2, w3, w4_words, w4_scales, offs, out
+):
+    nc = tc.nc
+    weights = (w1, w2, w3)
+    with ExitStack() as ctx:
+        keep = ctx.enter_context(tc.tile_pool(name="keep", bufs=1))
+        psum = ctx.enter_context(tc.psum_pool(name="psum", bufs=1))
+
+        offsets = keep.tile([P, PIECES * LIST_COLS], U16, name="offsets")
+        nc.sync.dma_start(offsets[:], offs)
+
+        w4_codes = keep.tile([P, N], U32, name="w4_codes", align_bytes=64)
+        w4_bytes = keep.tile([P, N], U8, name="w4_bytes", align_bytes=64)
+        nc.vector.memset(w4_bytes[:], 0)
+        nc.scalar.dma_start(
+            out=w4_codes[:].bitcast(I32), in_=w4_words[0].rearrange("p n t -> p (n t)").bitcast(I32)
+        )
+        for q in range(4):
+            nc.scalar.dma_start(
+                out=w4_bytes[32 * q : 32 * q + 4, :].bitcast(I32),
+                in_=w4_scales[0, 4 * q : 4 * q + 4, :].bitcast(I32),
+            )
+
+        x_rows = {}
+        for g in range(PASSES):
+            rows = xT[g * K_PASS : (g + 1) * K_PASS, :].rearrange("(p j) t -> p j t", j=PACK)
+            for j in range(PACK):
+                x_rows[g, j] = keep.tile([P, T], F32, name=f"x_rows_{g}_{j}")
+                nc.sync.dma_start(out=x_rows[g, j][:], in_=rows[:, j, :])
+        w_raw = {}
+        for d in range(PIECES):
+            for g in range(PASSES):
+                rows = weights[d][g * K_PASS : (g + 1) * K_PASS, :].rearrange("(p j) c -> p j c", j=PACK)
+                last = d == PIECES - 1 and g == PASSES - 1
+                parts = [(0, 2, LAST_SHARES[0]), (2, 4, LAST_SHARES[1])] if last else [(0, 4, SHARES[d, g])]
+                w_raw[d, g] = []
+                for j0, j1, share in parts:
+                    raw = keep.tile([P, j1 - j0, H], F32, name=f"w_raw_{d}_{g}_{j0}")
+                    nc.sync.dma_start(out=raw[:], in_=rows[:, j0:j1, :])
+                    w_raw[d, g].append((j0, j1, share, raw))
+
+        picked, x_grouped, x_codes, x_bytes = {}, {}, {}, {}
+        w_grouped, w_codes, w_bytes = {}, {}, {}
+        for g in range(PASSES):
+            for d in range(PIECES):
+                picked[g, d] = keep.tile([P, PACK, V], BF16, name=f"picked_{g}_{d}")
+                x_grouped[g, d] = keep.tile([P, V, PACK], BF16, name=f"x_grouped_{g}_{d}", align_bytes=64)
+                x_codes[g, d] = keep.tile([P, V], U32, name=f"x_codes_{g}_{d}", align_bytes=64)
+                x_bytes[g, d] = keep.tile([P, V], U8, name=f"x_bytes_{g}_{d}", align_bytes=64)
+                w_grouped[d, g] = keep.tile([P, PACK, P, PACK], BF16, name=f"w_grouped_{d}_{g}", align_bytes=64)
+                w_codes[d, g] = keep.tile([P, H], U32, name=f"w_codes_{d}_{g}", align_bytes=64)
+                w_bytes[d, g] = keep.tile([P, H], U8, name=f"w_bytes_{d}_{g}", align_bytes=64)
+        banks = {(d, h): psum.tile([P, PACK, HALF], F32, name=f"bank_{d}_{h}") for d in range(PIECES) for h in range(HALVES)}
+        first_sb = keep.tile([P, V, PACK], F32, name="first_sb")
+        first_two = keep.tile([P, V, PACK], F32, name="first_two")
+        z = keep.tile([P, V, PACK], BF16, name="z", align_bytes=64)
+        z_codes = keep.tile([P, V], U32, name="z_codes", align_bytes=64)
+        z_bytes = keep.tile([P, V], U8, name="z_bytes", align_bytes=64)
+        halves = [slice(h * HALF, (h + 1) * HALF) for h in range(HALVES)]
+
+        def gather(g, j):
+            for d in range(PIECES):
+                nc.vector.tensor_copy(
+                    out=picked[g, d][:, j, :],
+                    in_=x_rows[g, j][:].indirect(offsets[:, d * LIST_COLS : (d + 1) * LIST_COLS]),
+                )
+
+        def weave(g):
+            for d in range(PIECES):
+                nc.scalar.copy(
+                    out=x_grouped[g, d][:].rearrange("p (c i) j -> p c j i", i=4),
+                    in_=picked[g, d][:].rearrange("p j (c i) -> p c j i", i=4),
+                )
+
+        def quantize_x(g, d):
+            nc.vector.quantize_mx(
+                out=x_codes[g, d][:].bitcast(FP8X4),
+                scales=x_bytes[g, d][:],
+                in_=x_grouped[g, d][:].rearrange("p v j -> p (v j)"),
+            )
+
+        def round_w(d, g):
+            for j0, j1, share, raw in w_raw[d, g]:
+                dst = w_grouped[d, g][:].rearrange("p t m j -> p m j t")
+                src = raw[:].rearrange("p j (m t) -> p m j t", t=PACK)
+                if share:
+                    nc.scalar.copy(out=dst[:, :share, j0:j1, :], in_=src[:, :share])
+                nc.vector.tensor_copy(out=dst[:, share:, j0:j1, :], in_=src[:, share:])
+
+        def quantize_w(d, g, calls=1):
+            flat = w_grouped[d, g][:].rearrange("p t m j -> p (t m j)")
+            width = H // calls
+            for c in range(calls):
+                cols = slice(c * width, (c + 1) * width)
+                nc.vector.quantize_mx(
+                    out=w_codes[d, g][:, cols].bitcast(FP8X4),
+                    scales=w_bytes[d, g][:, cols],
+                    in_=flat[:, PACK * c * width : PACK * (c + 1) * width],
+                )
+
+        def multiply(d, g):
+            for h, cols in enumerate(halves):
+                for t in range(PACK):
+                    nc.tensor.matmul_mx(
+                        out=banks[d, h][:, t, :],
+                        lhsT=w_codes[d, g][:, t * P : (t + 1) * P].bitcast(FP8X4),
+                        lhsT_scale=w_bytes[d, g][:, t * P : (t + 1) * P],
+                        rhs=x_codes[g, d][:, cols].bitcast(FP8X4),
+                        rhs_scale=x_bytes[g, d][:, cols],
+                        start=(g == 0 and t == 0),
+                        stop=(g == PASSES - 1 and t == PACK - 1),
+                    )
+
+        def sums(d, h):
+            return banks[d, h][:].rearrange("p t v -> p v t")
+
+        def times(dst, d, factor, h):
+            nc.vector.tensor_tensor(out=dst[:, halves[h], :], in0=sums(d, h), in1=factor[:, halves[h], :], op=MULT)
+
+        for j in range(PACK):
+            gather(0, j)
+        weave(0)
+        for j in range(PACK):
+            gather(1, j)
+            if j < PIECES:
+                quantize_x(0, j)
+        weave(1)
+
+        quantize_x(1, 0)
+        round_w(0, 0)
+        quantize_x(1, 1)
+        quantize_w(0, 0)
+        multiply(0, 0)
+        round_w(0, 1)
+        quantize_x(1, 2)
+        quantize_w(0, 1)
+        multiply(0, 1)
+        round_w(1, 0)
+        quantize_w(1, 0)
+        multiply(1, 0)
+        round_w(1, 1)
+        for h, cols in enumerate(halves):
+            nc.scalar.copy(out=first_sb[:, cols, :], in_=sums(0, h))
+        quantize_w(1, 1, calls=PACK)
+        multiply(1, 1)
+        times(first_two, 1, first_sb, 0)
+        round_w(2, 0)
+        quantize_w(2, 0)
+        multiply(2, 0)
+        round_w(2, 1)
+        quantize_w(2, 1, calls=PACK)
+        multiply(2, 1)
+        times(first_two, 1, first_sb, 1)
+        for h in range(HALVES):
+            times(z, 2, first_two, h)
+
+        acc = [psum.tile([N, HALF], F32, name=f"acc_{h}") for h in range(HALVES)]
+        for h, cols in enumerate(halves):
+            nc.vector.quantize_mx(
+                out=z_codes[:, cols].bitcast(FP8X4),
+                scales=z_bytes[:, cols],
+                in_=z[:, cols, :].rearrange("p v t -> p (v t)"),
+            )
+            nc.tensor.matmul_mx(
+                out=acc[h][:],
+                lhsT=w4_codes[:].bitcast(FP8X4),
+                lhsT_scale=w4_bytes[:],
+                rhs=z_codes[:, cols].bitcast(FP8X4),
+                rhs_scale=z_bytes[:, cols],
+                start=True,
+                stop=True,
+            )
+        for h, cols in enumerate(halves):
+            result = keep.tile([N, HALF], F32, name=f"result_{h}")
+            nc.vector.tensor_scalar_max(out=result[:], in0=acc[h][:], scalar1=0.0)
+            nc.sync.dma_start(out=out[:, cols], in_=result[:])

@@ -22,8 +22,9 @@ PASSES = K // K_PASS
 HALF = 128
 HALVES = V // HALF
 LIST_COLS = V // 16
-SHARES = {(0, 0): 0, (0, 1): 64, (1, 0): 72, (1, 1): 48, (2, 0): 56}
-LAST_SHARES = (76, 44)
+SHARES = {(0, 0): 0, (1, 0): 80, (0, 1): 72, (1, 1): 64, (2, 0): 40}
+W_ORDER = ((0, 0), (1, 0), (0, 1), (1, 1), (2, 0))
+LAST_SHARES = (64, 20)
 
 
 def tile_picked_trilin_relu_e_kernel(
@@ -33,6 +34,7 @@ def tile_picked_trilin_relu_e_kernel(
     weights = (w1, w2, w3)
     with ExitStack() as ctx:
         keep = ctx.enter_context(tc.tile_pool(name="keep", bufs=1))
+        reuse = ctx.enter_context(tc.tile_pool(name="reuse", bufs=1))
         psum = ctx.enter_context(tc.psum_pool(name="psum", bufs=1))
 
         offsets = keep.tile([P, PIECES * LIST_COLS], U16, name="offsets")
@@ -57,16 +59,17 @@ def tile_picked_trilin_relu_e_kernel(
                 x_rows[g, j] = keep.tile([P, T], F32, name=f"x_rows_{g}_{j}")
                 nc.sync.dma_start(out=x_rows[g, j][:], in_=rows[:, j, :])
         w_raw = {}
-        for d in range(PIECES):
-            for g in range(PASSES):
-                rows = weights[d][g * K_PASS : (g + 1) * K_PASS, :].rearrange("(p j) c -> p j c", j=PACK)
-                last = d == PIECES - 1 and g == PASSES - 1
-                parts = [(0, 2, LAST_SHARES[0]), (2, 4, LAST_SHARES[1])] if last else [(0, 4, SHARES[d, g])]
-                w_raw[d, g] = []
-                for j0, j1, share in parts:
-                    raw = keep.tile([P, j1 - j0, H], F32, name=f"w_raw_{d}_{g}_{j0}")
-                    nc.sync.dma_start(out=raw[:], in_=rows[:, j0:j1, :])
-                    w_raw[d, g].append((j0, j1, share, raw))
+        for d, g in W_ORDER:
+            rows = weights[d][g * K_PASS : (g + 1) * K_PASS, :].rearrange("(p j) c -> p j c", j=PACK)
+            w_raw[d, g] = keep.tile([P, PACK, H], F32, name=f"w_raw_{d}_{g}")
+            nc.sync.dma_start(out=w_raw[d, g][:], in_=rows)
+        rows = w3[K_PASS:, :].rearrange("(p j) c -> p j c", j=PACK)
+        last_raw = [
+            keep.tile([P, PACK, H // 2], F32, name="last_raw_0"),
+            reuse.tile([P, PACK, H // 2], F32, name="last_raw_1", offset=0),
+        ]
+        for u in range(2):
+            nc.sync.dma_start(out=last_raw[u][:], in_=rows[:, :, u * (H // 2) : (u + 1) * (H // 2)])
 
         picked, x_grouped, x_codes, x_bytes = {}, {}, {}, {}
         w_grouped, w_codes, w_bytes = {}, {}, {}
@@ -81,7 +84,12 @@ def tile_picked_trilin_relu_e_kernel(
                 w_bytes[d, g] = keep.tile([P, H], U8, name=f"w_bytes_{d}_{g}", align_bytes=64)
         banks = {(d, h): psum.tile([P, PACK, HALF], F32, name=f"bank_{d}_{h}") for d in range(PIECES) for h in range(HALVES)}
         first_sb = keep.tile([P, V, PACK], F32, name="first_sb")
-        first_two = keep.tile([P, V, PACK], F32, name="first_two")
+        first_two = [
+            keep.tile([P, HALF, PACK], F32, name="first_two_0"),
+            reuse.tile([P, HALF, PACK], F32, name="first_two_1", offset=0),
+        ]
+        late_codes = reuse.tile([P, HALF], U32, name="late_codes", offset=2048, align_bytes=64)
+        late_bytes = keep.tile([P, HALF], U8, name="late_bytes", align_bytes=64)
         z = keep.tile([P, V, PACK], BF16, name="z", align_bytes=64)
         z_codes = keep.tile([P, V], U32, name="z_codes", align_bytes=64)
         z_bytes = keep.tile([P, V], U8, name="z_bytes", align_bytes=64)
@@ -101,50 +109,56 @@ def tile_picked_trilin_relu_e_kernel(
                     in_=picked[g, d][:].rearrange("p j (c i) -> p c j i", i=4),
                 )
 
-        def quantize_x(g, d):
+        def quantize_x(g, d, width=V):
             nc.vector.quantize_mx(
-                out=x_codes[g, d][:].bitcast(FP8X4),
-                scales=x_bytes[g, d][:],
-                in_=x_grouped[g, d][:].rearrange("p v j -> p (v j)"),
+                out=x_codes[g, d][:, :width].bitcast(FP8X4),
+                scales=x_bytes[g, d][:, :width],
+                in_=x_grouped[g, d][:, :width, :].rearrange("p v j -> p (v j)"),
             )
 
-        def round_w(d, g):
-            for j0, j1, share, raw in w_raw[d, g]:
-                dst = w_grouped[d, g][:].rearrange("p t m j -> p m j t")
-                src = raw[:].rearrange("p j (m t) -> p m j t", t=PACK)
-                if share:
-                    nc.scalar.copy(out=dst[:, :share, j0:j1, :], in_=src[:, :share])
-                nc.vector.tensor_copy(out=dst[:, share:, j0:j1, :], in_=src[:, share:])
+        def round_w(raw, d, g, m0, share):
+            src = raw[:].rearrange("p j (m t) -> p m t j", t=PACK)
+            count = src.shape[1]
+            dst = w_grouped[d, g][:].rearrange("p t m j -> p m t j")[:, m0 : m0 + count]
+            if share > 0:
+                nc.scalar.copy(out=dst[:, :share], in_=src[:, :share])
+            if share < count:
+                nc.vector.tensor_copy(out=dst[:, share:], in_=src[:, share:])
 
-        def quantize_w(d, g, calls=1):
-            flat = w_grouped[d, g][:].rearrange("p t m j -> p (t m j)")
-            width = H // calls
-            for c in range(calls):
-                cols = slice(c * width, (c + 1) * width)
+        def quantize_w(d, g):
+            nc.vector.quantize_mx(
+                out=w_codes[d, g][:].bitcast(FP8X4),
+                scales=w_bytes[d, g][:],
+                in_=w_grouped[d, g][:].rearrange("p t m j -> p (t m j)"),
+            )
+
+        def quantize_last(u):
+            for t in range(PACK):
+                cols = slice(t * P + u * P // 2, t * P + (u + 1) * P // 2)
                 nc.vector.quantize_mx(
-                    out=w_codes[d, g][:, cols].bitcast(FP8X4),
-                    scales=w_bytes[d, g][:, cols],
-                    in_=flat[:, PACK * c * width : PACK * (c + 1) * width],
+                    out=w_codes[2, 1][:, cols].bitcast(FP8X4),
+                    scales=w_bytes[2, 1][:, cols],
+                    in_=w_grouped[2, 1][:, t, u * P // 2 : (u + 1) * P // 2, :].rearrange("p m j -> p (m j)"),
                 )
 
         def multiply(d, g):
             for h, cols in enumerate(halves):
+                late = (d, g, h) == (2, 1, 1)
+                codes = late_codes[:] if late else x_codes[g, d][:, cols]
+                scales = late_bytes[:] if late else x_bytes[g, d][:, cols]
                 for t in range(PACK):
                     nc.tensor.matmul_mx(
                         out=banks[d, h][:, t, :],
                         lhsT=w_codes[d, g][:, t * P : (t + 1) * P].bitcast(FP8X4),
                         lhsT_scale=w_bytes[d, g][:, t * P : (t + 1) * P],
-                        rhs=x_codes[g, d][:, cols].bitcast(FP8X4),
-                        rhs_scale=x_bytes[g, d][:, cols],
+                        rhs=codes.bitcast(FP8X4),
+                        rhs_scale=scales,
                         start=(g == 0 and t == 0),
                         stop=(g == PASSES - 1 and t == PACK - 1),
                     )
 
         def sums(d, h):
             return banks[d, h][:].rearrange("p t v -> p v t")
-
-        def times(dst, d, factor, h):
-            nc.vector.tensor_tensor(out=dst[:, halves[h], :], in0=sums(d, h), in1=factor[:, halves[h], :], op=MULT)
 
         for j in range(PACK):
             gather(0, j)
@@ -156,32 +170,34 @@ def tile_picked_trilin_relu_e_kernel(
         weave(1)
 
         quantize_x(1, 0)
-        round_w(0, 0)
+        round_w(w_raw[0, 0], 0, 0, 0, SHARES[0, 0])
         quantize_x(1, 1)
+        quantize_x(1, 2, HALF)
         quantize_w(0, 0)
         multiply(0, 0)
-        round_w(0, 1)
-        quantize_x(1, 2)
-        quantize_w(0, 1)
-        multiply(0, 1)
-        round_w(1, 0)
-        quantize_w(1, 0)
-        multiply(1, 0)
-        round_w(1, 1)
+        for d, g in W_ORDER[1:4]:
+            round_w(w_raw[d, g], d, g, 0, SHARES[d, g])
+            quantize_w(d, g)
+            multiply(d, g)
         for h, cols in enumerate(halves):
             nc.scalar.copy(out=first_sb[:, cols, :], in_=sums(0, h))
-        quantize_w(1, 1, calls=PACK)
-        multiply(1, 1)
-        times(first_two, 1, first_sb, 0)
-        round_w(2, 0)
+        round_w(w_raw[2, 0], 2, 0, 0, SHARES[2, 0])
+        nc.vector.tensor_tensor(out=first_two[0][:], in0=sums(1, 0), in1=first_sb[:, halves[0], :], op=MULT)
         quantize_w(2, 0)
         multiply(2, 0)
-        round_w(2, 1)
-        quantize_w(2, 1, calls=PACK)
+        for u in range(2):
+            round_w(last_raw[u], 2, 1, u * P // 2, LAST_SHARES[u])
+        for u in range(2):
+            quantize_last(u)
+        nc.vector.quantize_mx(
+            out=late_codes[:].bitcast(FP8X4),
+            scales=late_bytes[:],
+            in_=x_grouped[1, 2][:, halves[1], :].rearrange("p v j -> p (v j)"),
+        )
         multiply(2, 1)
-        times(first_two, 1, first_sb, 1)
-        for h in range(HALVES):
-            times(z, 2, first_two, h)
+        nc.vector.tensor_tensor(out=first_two[1][:], in0=sums(1, 1), in1=first_sb[:, halves[1], :], op=MULT)
+        for h, cols in enumerate(halves):
+            nc.vector.tensor_tensor(out=z[:, cols, :], in0=sums(2, h), in1=first_two[h][:], op=MULT)
 
         acc = [psum.tile([N, HALF], F32, name=f"acc_{h}") for h in range(HALVES)]
         for h, cols in enumerate(halves):

@@ -83,10 +83,10 @@ def tile_picked_trilin_relu_e_kernel(
                 w_codes[d, g] = keep.tile([P, H], U32, name=f"w_codes_{d}_{g}", align_bytes=64)
                 w_bytes[d, g] = keep.tile([P, H], U8, name=f"w_bytes_{d}_{g}", align_bytes=64)
         banks = {(d, h): psum.tile([P, PACK, HALF], F32, name=f"bank_{d}_{h}") for d in range(PIECES) for h in range(HALVES)}
-        first_sb = keep.tile([P, V, PACK], F32, name="first_sb")
+        first_sb = [keep.tile([P, PACK, HALF], F32, name=f"first_sb_{h}") for h in range(HALVES)]
         first_two = [
-            keep.tile([P, HALF, PACK], F32, name="first_two_0"),
-            reuse.tile([P, HALF, PACK], F32, name="first_two_1", offset=0),
+            keep.tile([P, PACK, HALF], F32, name="first_two_0"),
+            reuse.tile([P, PACK, HALF], F32, name="first_two_1", offset=0),
         ]
         late_codes = reuse.tile([P, HALF], U32, name="late_codes", offset=2048, align_bytes=64)
         late_bytes = keep.tile([P, HALF], U8, name="late_bytes", align_bytes=64)
@@ -117,13 +117,13 @@ def tile_picked_trilin_relu_e_kernel(
             )
 
         def round_w(raw, d, g, m0, share):
-            src = raw[:].rearrange("p j (m t) -> p m t j", t=PACK)
-            count = src.shape[1]
-            dst = w_grouped[d, g][:].rearrange("p t m j -> p m t j")[:, m0 : m0 + count]
+            src = raw[:].rearrange("p j (m u e) -> p u m j e", u=2, e=2)
+            count = src.shape[2]
+            dst = w_grouped[d, g][:].rearrange("p (u e) m j -> p u m j e", e=2)[:, :, m0 : m0 + count]
             if share > 0:
-                nc.scalar.copy(out=dst[:, :share], in_=src[:, :share])
+                nc.scalar.copy(out=dst[:, :, :share], in_=src[:, :, :share])
             if share < count:
-                nc.vector.tensor_copy(out=dst[:, share:], in_=src[:, share:])
+                nc.vector.tensor_copy(out=dst[:, :, share:], in_=src[:, :, share:])
 
         def quantize_w(d, g):
             nc.vector.quantize_mx(
@@ -157,9 +157,6 @@ def tile_picked_trilin_relu_e_kernel(
                         stop=(g == PASSES - 1 and t == PACK - 1),
                     )
 
-        def sums(d, h):
-            return banks[d, h][:].rearrange("p t v -> p v t")
-
         for j in range(PACK):
             gather(0, j)
         weave(0)
@@ -179,10 +176,10 @@ def tile_picked_trilin_relu_e_kernel(
             round_w(w_raw[d, g], d, g, 0, SHARES[d, g])
             quantize_w(d, g)
             multiply(d, g)
-        for h, cols in enumerate(halves):
-            nc.scalar.copy(out=first_sb[:, cols, :], in_=sums(0, h))
+        for h in range(HALVES):
+            nc.scalar.copy(out=first_sb[h][:], in_=banks[0, h][:])
         round_w(w_raw[2, 0], 2, 0, 0, SHARES[2, 0])
-        nc.vector.tensor_tensor(out=first_two[0][:], in0=sums(1, 0), in1=first_sb[:, halves[0], :], op=MULT)
+        nc.vector.tensor_tensor(out=first_two[0][:], in0=banks[1, 0][:], in1=first_sb[0][:], op=MULT)
         quantize_w(2, 0)
         multiply(2, 0)
         for u in range(2):
@@ -195,9 +192,14 @@ def tile_picked_trilin_relu_e_kernel(
             in_=x_grouped[1, 2][:, halves[1], :].rearrange("p v j -> p (v j)"),
         )
         multiply(2, 1)
-        nc.vector.tensor_tensor(out=first_two[1][:], in0=sums(1, 1), in1=first_sb[:, halves[1], :], op=MULT)
+        nc.vector.tensor_tensor(out=first_two[1][:], in0=banks[1, 1][:], in1=first_sb[1][:], op=MULT)
         for h, cols in enumerate(halves):
-            nc.vector.tensor_tensor(out=z[:, cols, :], in0=sums(2, h), in1=first_two[h][:], op=MULT)
+            nc.vector.tensor_tensor(
+                out=z[:, cols, :].rearrange("p (c e) t -> p c t e", e=2),
+                in0=banks[2, h][:].rearrange("p t (c e) -> p c t e", e=2),
+                in1=first_two[h][:].rearrange("p t (c e) -> p c t e", e=2),
+                op=MULT,
+            )
 
         acc = [psum.tile([N, HALF], F32, name=f"acc_{h}") for h in range(HALVES)]
         for h, cols in enumerate(halves):

@@ -75,7 +75,7 @@ def tile_picked_trilin_relu_e_kernel(
         w_grouped, w_codes, w_bytes = {}, {}, {}
         for g in range(PASSES):
             for d in range(PIECES):
-                picked[g, d] = keep.tile([P, PACK, V], BF16, name=f"picked_{g}_{d}")
+                picked[g, d] = keep.tile([P, PACK, V], F32, name=f"picked_{g}_{d}")
                 x_grouped[g, d] = keep.tile([P, V, PACK], BF16, name=f"x_grouped_{g}_{d}", align_bytes=64)
                 x_codes[g, d] = keep.tile([P, V], U32, name=f"x_codes_{g}_{d}", align_bytes=64)
                 x_bytes[g, d] = keep.tile([P, V], U8, name=f"x_bytes_{g}_{d}", align_bytes=64)

@@ -22,9 +22,28 @@ PASSES = K // K_PASS
 HALF = 128
 HALVES = V // HALF
 LIST_COLS = V // 16
-SHARES = {(0, 0): 0, (1, 0): 80, (0, 1): 72, (1, 1): 64, (2, 0): 40}
-W_ORDER = ((0, 0), (1, 0), (0, 1), (1, 1), (2, 0))
-LAST_SHARES = (64, 20)
+QUADRANT = 32
+
+W1_FIRST, W2_FIRST, W1_LAST, W2_LAST, W3_FIRST, W3_LAST = (0, 0), (1, 0), (0, 1), (1, 1), (2, 0), (2, 1)
+WHOLE_LOADS = (W1_FIRST, W2_FIRST, W1_LAST, W2_LAST, W3_FIRST)
+M_HALF = P // 2
+
+SHARE_EARLY = 76
+SHARE_W2_LAST = 56
+SHARE_W3_FIRST = 40
+SHARE_W3_LAST = (48, 36)
+SCALAR_SHARE = {
+    W1_FIRST: 0,
+    W2_FIRST: SHARE_EARLY,
+    W1_LAST: SHARE_EARLY,
+    W2_LAST: SHARE_W2_LAST,
+    W3_FIRST: SHARE_W3_FIRST,
+}
+
+LAST_RAW_AT = 0
+FIRST_RAW_AT = PACK * (H // 2) * 4
+BANK_BYTES = PACK * HALF * 4
+X_CODES_BYTES = V * 4
 
 
 def tile_picked_trilin_relu_e_kernel(
@@ -32,25 +51,16 @@ def tile_picked_trilin_relu_e_kernel(
 ):
     nc = tc.nc
     weights = (w1, w2, w3)
+    halves = [slice(h * HALF, (h + 1) * HALF) for h in range(HALVES)]
     with ExitStack() as ctx:
         keep = ctx.enter_context(tc.tile_pool(name="keep", bufs=1))
         reuse = ctx.enter_context(tc.tile_pool(name="reuse", bufs=1))
         psum = ctx.enter_context(tc.psum_pool(name="psum", bufs=1))
 
         offsets = keep.tile([P, PIECES * LIST_COLS], U16, name="offsets")
-        nc.sync.dma_start(offsets[:], offs)
-
         w4_codes = keep.tile([P, N], U32, name="w4_codes", align_bytes=64)
         w4_bytes = keep.tile([P, N], U8, name="w4_bytes", align_bytes=64)
         nc.vector.memset(w4_bytes[:], 0)
-        nc.scalar.dma_start(
-            out=w4_codes[:].bitcast(I32), in_=w4_words[0].rearrange("p n t -> p (n t)").bitcast(I32)
-        )
-        for q in range(4):
-            nc.scalar.dma_start(
-                out=w4_bytes[32 * q : 32 * q + 4, :].bitcast(I32),
-                in_=w4_scales[0, 4 * q : 4 * q + 4, :].bitcast(I32),
-            )
 
         x_rows = {}
         for g in range(PASSES):
@@ -58,62 +68,89 @@ def tile_picked_trilin_relu_e_kernel(
             for j in range(PACK):
                 x_rows[g, j] = keep.tile([P, T], F32, name=f"x_rows_{g}_{j}")
                 nc.sync.dma_start(out=x_rows[g, j][:], in_=rows[:, j, :])
+                if (g, j) == (0, 0):
+                    nc.sync.dma_start(offsets[:], offs)
+
+        def weight_rows(d, g):
+            return weights[d][g * K_PASS : (g + 1) * K_PASS, :].rearrange("(p j) c -> p j c", j=PACK)
+
         w_raw = {}
-        for d, g in W_ORDER:
-            rows = weights[d][g * K_PASS : (g + 1) * K_PASS, :].rearrange("(p j) c -> p j c", j=PACK)
-            w_raw[d, g] = keep.tile([P, PACK, H], F32, name=f"w_raw_{d}_{g}")
-            nc.sync.dma_start(out=w_raw[d, g][:], in_=rows)
-        rows = w3[K_PASS:, :].rearrange("(p j) c -> p j c", j=PACK)
+        for d, g in WHOLE_LOADS:
+            if (d, g) == W1_FIRST:
+                w_raw[d, g] = reuse.tile([P, PACK, H], F32, name="w_raw_first", offset=FIRST_RAW_AT)
+            else:
+                w_raw[d, g] = keep.tile([P, PACK, H], F32, name=f"w_raw_{d}_{g}")
+            nc.sync.dma_start(out=w_raw[d, g][:], in_=weight_rows(d, g))
         last_raw = [
             keep.tile([P, PACK, H // 2], F32, name="last_raw_0"),
-            reuse.tile([P, PACK, H // 2], F32, name="last_raw_1", offset=0),
+            reuse.tile([P, PACK, H // 2], F32, name="last_raw_1", offset=LAST_RAW_AT),
         ]
-        for u in range(2):
-            nc.sync.dma_start(out=last_raw[u][:], in_=rows[:, :, u * (H // 2) : (u + 1) * (H // 2)])
+        for part in range(2):
+            channels = slice(part * (H // 2), (part + 1) * (H // 2))
+            nc.sync.dma_start(out=last_raw[part][:], in_=weight_rows(*W3_LAST)[:, :, channels])
+
+        nc.sync.dma_start(
+            out=w4_codes[:].bitcast(I32), in_=w4_words[0].rearrange("p n t -> p (n t)").bitcast(I32)
+        )
+        for q in range(P // QUADRANT):
+            nc.sync.dma_start(
+                out=w4_bytes[QUADRANT * q : QUADRANT * q + 4, :].bitcast(I32),
+                in_=w4_scales[0, 4 * q : 4 * q + 4, :].bitcast(I32),
+            )
 
         picked, x_grouped, x_codes, x_bytes = {}, {}, {}, {}
         w_grouped, w_codes, w_bytes = {}, {}, {}
         for g in range(PASSES):
             for d in range(PIECES):
-                picked[g, d] = keep.tile([P, PACK, V], F32, name=f"picked_{g}_{d}")
+                for u in range(2):
+                    picked[g, d, u] = keep.tile([P, 2, V], F32, name=f"picked_{g}_{d}_{u}")
                 x_grouped[g, d] = keep.tile([P, V, PACK], BF16, name=f"x_grouped_{g}_{d}", align_bytes=64)
-                x_codes[g, d] = keep.tile([P, V], U32, name=f"x_codes_{g}_{d}", align_bytes=64)
+                if g == 1 and d > 0:
+                    x_codes[g, d] = reuse.tile(
+                        [P, V], U32, name=f"x_codes_{g}_{d}", align_bytes=64, offset=FIRST_RAW_AT + X_CODES_BYTES * d
+                    )
+                else:
+                    x_codes[g, d] = keep.tile([P, V], U32, name=f"x_codes_{g}_{d}", align_bytes=64)
                 x_bytes[g, d] = keep.tile([P, V], U8, name=f"x_bytes_{g}_{d}", align_bytes=64)
                 w_grouped[d, g] = keep.tile([P, PACK, P, PACK], BF16, name=f"w_grouped_{d}_{g}", align_bytes=64)
                 w_codes[d, g] = keep.tile([P, H], U32, name=f"w_codes_{d}_{g}", align_bytes=64)
                 w_bytes[d, g] = keep.tile([P, H], U8, name=f"w_bytes_{d}_{g}", align_bytes=64)
-        banks = {(d, h): psum.tile([P, PACK, HALF], F32, name=f"bank_{d}_{h}") for d in range(PIECES) for h in range(HALVES)}
-        first_sb = [keep.tile([P, PACK, HALF], F32, name=f"first_sb_{h}") for h in range(HALVES)]
+        banks = {
+            (d, h): psum.tile([P, PACK, HALF], F32, name=f"bank_{d}_{h}") for d in range(PIECES) for h in range(HALVES)
+        }
+        first = [keep.tile([P, PACK, HALF], F32, name=f"first_{h}") for h in range(HALVES)]
         first_two = [
             keep.tile([P, PACK, HALF], F32, name="first_two_0"),
-            reuse.tile([P, PACK, HALF], F32, name="first_two_1", offset=0),
+            reuse.tile([P, PACK, HALF], F32, name="first_two_1", offset=LAST_RAW_AT),
         ]
-        late_codes = reuse.tile([P, HALF], U32, name="late_codes", offset=2048, align_bytes=64)
+        late_codes = reuse.tile([P, HALF], U32, name="late_codes", offset=LAST_RAW_AT + BANK_BYTES, align_bytes=64)
         late_bytes = keep.tile([P, HALF], U8, name="late_bytes", align_bytes=64)
         z = keep.tile([P, V, PACK], BF16, name="z", align_bytes=64)
         z_codes = keep.tile([P, V], U32, name="z_codes", align_bytes=64)
         z_bytes = keep.tile([P, V], U8, name="z_bytes", align_bytes=64)
-        halves = [slice(h * HALF, (h + 1) * HALF) for h in range(HALVES)]
 
         def gather(g, j):
             for d in range(PIECES):
                 nc.vector.tensor_copy(
-                    out=picked[g, d][:, j, :],
+                    out=picked[g, d, j // 2][:, j % 2, :],
                     in_=x_rows[g, j][:].indirect(offsets[:, d * LIST_COLS : (d + 1) * LIST_COLS]),
                 )
 
-        def weave(g):
+        def interleave(g, u):
             for d in range(PIECES):
                 nc.scalar.copy(
-                    out=x_grouped[g, d][:].rearrange("p (c i) j -> p c j i", i=4),
-                    in_=picked[g, d][:].rearrange("p j (c i) -> p c j i", i=4),
+                    out=x_grouped[g, d][:, :, 2 * u : 2 * u + 2],
+                    in_=picked[g, d, u][:].rearrange("p e v -> p v e"),
                 )
 
-        def quantize_x(g, d, width=V):
-            nc.vector.quantize_mx(
-                out=x_codes[g, d][:, :width].bitcast(FP8X4),
-                scales=x_bytes[g, d][:, :width],
-                in_=x_grouped[g, d][:, :width, :].rearrange("p v j -> p (v j)"),
+        def quantize(codes, scale_bytes, grouped):
+            nc.vector.quantize_mx(out=codes.bitcast(FP8X4), scales=scale_bytes, in_=grouped)
+
+        def quantize_x(g, d, entries=V):
+            quantize(
+                x_codes[g, d][:, :entries],
+                x_bytes[g, d][:, :entries],
+                x_grouped[g, d][:, :entries, :].rearrange("p v j -> p (v j)"),
             )
 
         def round_w(raw, d, g, m0, share):
@@ -122,77 +159,74 @@ def tile_picked_trilin_relu_e_kernel(
             dst = w_grouped[d, g][:].rearrange("p (u e) m j -> p u m j e", e=2)[:, :, m0 : m0 + count]
             if share > 0:
                 nc.scalar.copy(out=dst[:, :, :share], in_=src[:, :, :share])
-            if share < count:
-                nc.vector.tensor_copy(out=dst[:, :, share:], in_=src[:, :, share:])
+            nc.vector.tensor_copy(out=dst[:, :, share:], in_=src[:, :, share:])
 
         def quantize_w(d, g):
-            nc.vector.quantize_mx(
-                out=w_codes[d, g][:].bitcast(FP8X4),
-                scales=w_bytes[d, g][:],
-                in_=w_grouped[d, g][:].rearrange("p t m j -> p (t m j)"),
-            )
+            quantize(w_codes[d, g][:], w_bytes[d, g][:], w_grouped[d, g][:].rearrange("p t m j -> p (t m j)"))
 
-        def quantize_last(u):
+        def quantize_last(part):
             for t in range(PACK):
-                cols = slice(t * P + u * P // 2, t * P + (u + 1) * P // 2)
-                nc.vector.quantize_mx(
-                    out=w_codes[2, 1][:, cols].bitcast(FP8X4),
-                    scales=w_bytes[2, 1][:, cols],
-                    in_=w_grouped[2, 1][:, t, u * P // 2 : (u + 1) * P // 2, :].rearrange("p m j -> p (m j)"),
+                cols = slice(t * P + part * M_HALF, t * P + (part + 1) * M_HALF)
+                quantize(
+                    w_codes[W3_LAST][:, cols],
+                    w_bytes[W3_LAST][:, cols],
+                    w_grouped[W3_LAST][:, t, part * M_HALF : (part + 1) * M_HALF, :].rearrange("p m j -> p (m j)"),
                 )
 
         def multiply(d, g):
             for h, cols in enumerate(halves):
-                late = (d, g, h) == (2, 1, 1)
+                late = (d, g) == W3_LAST and h == 1
                 codes = late_codes[:] if late else x_codes[g, d][:, cols]
-                scales = late_bytes[:] if late else x_bytes[g, d][:, cols]
+                scale_bytes = late_bytes[:] if late else x_bytes[g, d][:, cols]
                 for t in range(PACK):
                     nc.tensor.matmul_mx(
                         out=banks[d, h][:, t, :],
                         lhsT=w_codes[d, g][:, t * P : (t + 1) * P].bitcast(FP8X4),
                         lhsT_scale=w_bytes[d, g][:, t * P : (t + 1) * P],
                         rhs=codes.bitcast(FP8X4),
-                        rhs_scale=scales,
+                        rhs_scale=scale_bytes,
                         start=(g == 0 and t == 0),
                         stop=(g == PASSES - 1 and t == PACK - 1),
                     )
 
+        def times_second(h):
+            nc.vector.tensor_tensor(out=first_two[h][:], in0=banks[1, h][:], in1=first[h][:], op=MULT)
+
         for j in range(PACK):
             gather(0, j)
-        weave(0)
+            if j % 2:
+                interleave(0, j // 2)
         for j in range(PACK):
             gather(1, j)
             if j < PIECES:
                 quantize_x(0, j)
-        weave(1)
+            if j % 2:
+                interleave(1, j // 2)
 
         quantize_x(1, 0)
-        round_w(w_raw[0, 0], 0, 0, 0, SHARES[0, 0])
+        round_w(w_raw[W1_FIRST], *W1_FIRST, 0, SCALAR_SHARE[W1_FIRST])
         quantize_x(1, 1)
         quantize_x(1, 2, HALF)
-        quantize_w(0, 0)
-        multiply(0, 0)
-        for d, g in W_ORDER[1:4]:
-            round_w(w_raw[d, g], d, g, 0, SHARES[d, g])
+        quantize_w(*W1_FIRST)
+        multiply(*W1_FIRST)
+        for d, g in (W2_FIRST, W1_LAST, W2_LAST):
+            round_w(w_raw[d, g], d, g, 0, SCALAR_SHARE[d, g])
             quantize_w(d, g)
             multiply(d, g)
         for h in range(HALVES):
-            nc.scalar.copy(out=first_sb[h][:], in_=banks[0, h][:])
-        round_w(w_raw[2, 0], 2, 0, 0, SHARES[2, 0])
-        nc.vector.tensor_tensor(out=first_two[0][:], in0=banks[1, 0][:], in1=first_sb[0][:], op=MULT)
-        quantize_w(2, 0)
-        multiply(2, 0)
-        for u in range(2):
-            round_w(last_raw[u], 2, 1, u * P // 2, LAST_SHARES[u])
-        for u in range(2):
-            quantize_last(u)
-        nc.vector.quantize_mx(
-            out=late_codes[:].bitcast(FP8X4),
-            scales=late_bytes[:],
-            in_=x_grouped[1, 2][:, halves[1], :].rearrange("p v j -> p (v j)"),
-        )
-        multiply(2, 1)
-        nc.vector.tensor_tensor(out=first_two[1][:], in0=banks[1, 1][:], in1=first_sb[1][:], op=MULT)
+            nc.scalar.copy(out=first[h][:], in_=banks[0, h][:])
+
+        round_w(w_raw[W3_FIRST], *W3_FIRST, 0, SCALAR_SHARE[W3_FIRST])
+        times_second(0)
+        quantize_w(*W3_FIRST)
+        multiply(*W3_FIRST)
+        for part in range(2):
+            round_w(last_raw[part], *W3_LAST, part * M_HALF, SHARE_W3_LAST[part])
+        for part in range(2):
+            quantize_last(part)
+        quantize(late_codes[:], late_bytes[:], x_grouped[1, 2][:, halves[1], :].rearrange("p v j -> p (v j)"))
+        multiply(*W3_LAST)
+        times_second(1)
         for h, cols in enumerate(halves):
             nc.vector.tensor_tensor(
                 out=z[:, cols, :].rearrange("p (c e) t -> p c t e", e=2),
@@ -203,11 +237,7 @@ def tile_picked_trilin_relu_e_kernel(
 
         acc = [psum.tile([N, HALF], F32, name=f"acc_{h}") for h in range(HALVES)]
         for h, cols in enumerate(halves):
-            nc.vector.quantize_mx(
-                out=z_codes[:, cols].bitcast(FP8X4),
-                scales=z_bytes[:, cols],
-                in_=z[:, cols, :].rearrange("p v t -> p (v t)"),
-            )
+            quantize(z_codes[:, cols], z_bytes[:, cols], z[:, cols, :].rearrange("p v t -> p (v t)"))
             nc.tensor.matmul_mx(
                 out=acc[h][:],
                 lhsT=w4_codes[:].bitcast(FP8X4),

from contextlib import ExitStack

import concourse.mybir as mybir

K, T, V, H, N = 1024, 2048, 256, 512, 128
PIECES = 3
FLOPS = 2 * PIECES * K * H * V + 2 * H * N * V

F32 = mybir.dt.float32
BF16 = mybir.dt.bfloat16
I32 = mybir.dt.int32
U32 = mybir.dt.uint32
U16 = mybir.dt.uint16
U8 = mybir.dt.uint8
FP8X4 = mybir.dt.float8_e4m3fn_x4
MULT = mybir.AluOpType.mult

P = 128
PACK = 4
K_PASS = P * PACK
PASSES = K // K_PASS
HALF = 128
HALVES = V // HALF
LIST_COLS = V // 16
QUADRANT = 32

W1_FIRST, W2_FIRST, W1_LAST, W2_LAST, W3_FIRST, W3_LAST = (0, 0), (1, 0), (0, 1), (1, 1), (2, 0), (2, 1)
WHOLE_LOADS = (W1_FIRST, W2_FIRST, W1_LAST, W2_LAST, W3_FIRST)
M_HALF = P // 2

SHARE_EARLY = 76
SHARE_W2_LAST = 56
SHARE_W3_FIRST = 40
SHARE_W3_LAST = (48, 36)
SCALAR_SHARE = {
    W1_FIRST: 0,
    W2_FIRST: SHARE_EARLY,
    W1_LAST: SHARE_EARLY,
    W2_LAST: SHARE_W2_LAST,
    W3_FIRST: SHARE_W3_FIRST,
}

LAST_RAW_AT = 0
FIRST_RAW_AT = PACK * (H // 2) * 4
BANK_BYTES = PACK * HALF * 4
X_CODES_BYTES = V * 4


def tile_picked_trilin_relu_e_kernel(
    tc, xT, w1, w2, w3, w4_words, w4_scales, offs, out
):
    nc = tc.nc
    weights = (w1, w2, w3)
    halves = [slice(h * HALF, (h + 1) * HALF) for h in range(HALVES)]
    with ExitStack() as ctx:
        keep = ctx.enter_context(tc.tile_pool(name="keep", bufs=1))
        reuse = ctx.enter_context(tc.tile_pool(name="reuse", bufs=1))
        psum = ctx.enter_context(tc.psum_pool(name="psum", bufs=1))

        offsets = keep.tile([P, PIECES * LIST_COLS], U16, name="offsets")
        w4_codes = keep.tile([P, N], U32, name="w4_codes", align_bytes=64)
        w4_bytes = keep.tile([P, N], U8, name="w4_bytes", align_bytes=64)
        nc.vector.memset(w4_bytes[:], 0)

        x_rows = {}
        for g in range(PASSES):
            rows = xT[g * K_PASS : (g + 1) * K_PASS, :].rearrange("(p j) t -> p j t", j=PACK)
            for j in range(PACK):
                x_rows[g, j] = keep.tile([P, T], F32, name=f"x_rows_{g}_{j}")
                nc.sync.dma_start(out=x_rows[g, j][:], in_=rows[:, j, :])
                if (g, j) == (0, 0):
                    nc.sync.dma_start(offsets[:], offs)

        def weight_rows(d, g):
            return weights[d][g * K_PASS : (g + 1) * K_PASS, :].rearrange("(p j) c -> p j c", j=PACK)

        w_raw = {}
        for d, g in WHOLE_LOADS:
            if (d, g) == W1_FIRST:
                w_raw[d, g] = reuse.tile([P, PACK, H], F32, name="w_raw_first", offset=FIRST_RAW_AT)
            else:
                w_raw[d, g] = keep.tile([P, PACK, H], F32, name=f"w_raw_{d}_{g}")
            nc.sync.dma_start(out=w_raw[d, g][:], in_=weight_rows(d, g))
        last_raw = [
            keep.tile([P, PACK, H // 2], F32, name="last_raw_0"),
            reuse.tile([P, PACK, H // 2], F32, name="last_raw_1", offset=LAST_RAW_AT),
        ]
        for part in range(2):
            channels = slice(part * (H // 2), (part + 1) * (H // 2))
            nc.sync.dma_start(out=last_raw[part][:], in_=weight_rows(*W3_LAST)[:, :, channels])

        nc.sync.dma_start(
            out=w4_codes[:].bitcast(I32), in_=w4_words[0].rearrange("p n t -> p (n t)").bitcast(I32)
        )
        for q in range(P // QUADRANT):
            nc.sync.dma_start(
                out=w4_bytes[QUADRANT * q : QUADRANT * q + 4, :].bitcast(I32),
                in_=w4_scales[0, 4 * q : 4 * q + 4, :].bitcast(I32),
            )

        picked, x_grouped, x_codes, x_bytes = {}, {}, {}, {}
        w_grouped, w_codes, w_bytes = {}, {}, {}
        for g in range(PASSES):
            for d in range(PIECES):
                for u in range(2):
                    picked[g, d, u] = keep.tile([P, 2, V], F32, name=f"picked_{g}_{d}_{u}")
                x_grouped[g, d] = keep.tile([P, V, PACK], BF16, name=f"x_grouped_{g}_{d}", align_bytes=64)
                if g == 1 and d > 0:
                    x_codes[g, d] = reuse.tile(
                        [P, V], U32, name=f"x_codes_{g}_{d}", align_bytes=64, offset=FIRST_RAW_AT + X_CODES_BYTES * d
                    )
                else:
                    x_codes[g, d] = keep.tile([P, V], U32, name=f"x_codes_{g}_{d}", align_bytes=64)
                x_bytes[g, d] = keep.tile([P, V], U8, name=f"x_bytes_{g}_{d}", align_bytes=64)
                w_grouped[d, g] = keep.tile([P, PACK, P, PACK], BF16, name=f"w_grouped_{d}_{g}", align_bytes=64)
                w_codes[d, g] = keep.tile([P, H], U32, name=f"w_codes_{d}_{g}", align_bytes=64)
                w_bytes[d, g] = keep.tile([P, H], U8, name=f"w_bytes_{d}_{g}", align_bytes=64)
        banks = {
            (d, h): psum.tile([P, PACK, HALF], F32, name=f"bank_{d}_{h}") for d in range(PIECES) for h in range(HALVES)
        }
        first = [keep.tile([P, PACK, HALF], F32, name=f"first_{h}") for h in range(HALVES)]
        first_two = [
            keep.tile([P, PACK, HALF], F32, name="first_two_0"),
            reuse.tile([P, PACK, HALF], F32, name="first_two_1", offset=LAST_RAW_AT),
        ]
        late_codes = reuse.tile([P, HALF], U32, name="late_codes", offset=LAST_RAW_AT + BANK_BYTES, align_bytes=64)
        late_bytes = keep.tile([P, HALF], U8, name="late_bytes", align_bytes=64)
        z = keep.tile([P, V, PACK], BF16, name="z", align_bytes=64)
        z_codes = keep.tile([P, V], U32, name="z_codes", align_bytes=64)
        z_bytes = keep.tile([P, V], U8, name="z_bytes", align_bytes=64)

        def gather(g, j):
            for d in range(PIECES):
                nc.vector.tensor_copy(
                    out=picked[g, d, j // 2][:, j % 2, :],
                    in_=x_rows[g, j][:].indirect(offsets[:, d * LIST_COLS : (d + 1) * LIST_COLS]),
                )

        def interleave(g, u):
            for d in range(PIECES):
                nc.scalar.copy(
                    out=x_grouped[g, d][:, :, 2 * u : 2 * u + 2],
                    in_=picked[g, d, u][:].rearrange("p e v -> p v e"),
                )

        def quantize(codes, scale_bytes, grouped):
            nc.vector.quantize_mx(out=codes.bitcast(FP8X4), scales=scale_bytes, in_=grouped)

        def quantize_x(g, d, entries=V):
            quantize(
                x_codes[g, d][:, :entries],
                x_bytes[g, d][:, :entries],
                x_grouped[g, d][:, :entries, :].rearrange("p v j -> p (v j)"),
            )

        def round_w(raw, d, g, m0, share):
            src = raw[:].rearrange("p j (m u e) -> p u m j e", u=2, e=2)
            count = src.shape[2]
            dst = w_grouped[d, g][:].rearrange("p (u e) m j -> p u m j e", e=2)[:, :, m0 : m0 + count]
            if share > 0:
                nc.scalar.copy(out=dst[:, :, :share], in_=src[:, :, :share])
            nc.vector.tensor_copy(out=dst[:, :, share:], in_=src[:, :, share:])

        def quantize_w(d, g):
            quantize(w_codes[d, g][:], w_bytes[d, g][:], w_grouped[d, g][:].rearrange("p t m j -> p (t m j)"))

        def quantize_last(part):
            for t in range(PACK):
                cols = slice(t * P + part * M_HALF, t * P + (part + 1) * M_HALF)
                quantize(
                    w_codes[W3_LAST][:, cols],
                    w_bytes[W3_LAST][:, cols],
                    w_grouped[W3_LAST][:, t, part * M_HALF : (part + 1) * M_HALF, :].rearrange("p m j -> p (m j)"),
                )

        def multiply(d, g):
            for h, cols in enumerate(halves):
                late = (d, g) == W3_LAST and h == 1
                codes = late_codes[:] if late else x_codes[g, d][:, cols]
                scale_bytes = late_bytes[:] if late else x_bytes[g, d][:, cols]
                for t in range(PACK):
                    nc.tensor.matmul_mx(
                        out=banks[d, h][:, t, :],
                        lhsT=w_codes[d, g][:, t * P : (t + 1) * P].bitcast(FP8X4),
                        lhsT_scale=w_bytes[d, g][:, t * P : (t + 1) * P],
                        rhs=codes.bitcast(FP8X4),
                        rhs_scale=scale_bytes,
                        start=(g == 0 and t == 0),
                        stop=(g == PASSES - 1 and t == PACK - 1),
                    )

        def times_second(h):
            nc.vector.tensor_tensor(out=first_two[h][:], in0=banks[1, h][:], in1=first[h][:], op=MULT)

        for j in range(PACK):
            gather(0, j)
            if j % 2:
                interleave(0, j // 2)
        for j in range(PACK):
            gather(1, j)
            if j < PIECES:
                quantize_x(0, j)
            if j % 2:
                interleave(1, j // 2)

        quantize_x(1, 0)
        round_w(w_raw[W1_FIRST], *W1_FIRST, 0, SCALAR_SHARE[W1_FIRST])
        quantize_x(1, 1)
        quantize_x(1, 2, HALF)
        quantize_w(*W1_FIRST)
        multiply(*W1_FIRST)
        for d, g in (W2_FIRST, W1_LAST, W2_LAST):
            round_w(w_raw[d, g], d, g, 0, SCALAR_SHARE[d, g])
            quantize_w(d, g)
            multiply(d, g)
        for h in range(HALVES):
            nc.scalar.copy(out=first[h][:], in_=banks[0, h][:])

        round_w(w_raw[W3_FIRST], *W3_FIRST, 0, SCALAR_SHARE[W3_FIRST])
        times_second(0)
        quantize_w(*W3_FIRST)
        multiply(*W3_FIRST)
        for part in range(2):
            round_w(last_raw[part], *W3_LAST, part * M_HALF, SHARE_W3_LAST[part])
        for part in range(2):
            quantize_last(part)
        quantize(late_codes[:], late_bytes[:], x_grouped[1, 2][:, halves[1], :].rearrange("p v j -> p (v j)"))
        multiply(*W3_LAST)
        times_second(1)
        for h, cols in enumerate(halves):
            nc.vector.tensor_tensor(
                out=z[:, cols, :].rearrange("p (c e) t -> p c t e", e=2),
                in0=banks[2, h][:].rearrange("p t (c e) -> p c t e", e=2),
                in1=first_two[h][:].rearrange("p t (c e) -> p c t e", e=2),
                op=MULT,
            )

        acc = [psum.tile([N, HALF], F32, name=f"acc_{h}") for h in range(HALVES)]
        for h, cols in enumerate(halves):
            quantize(z_codes[:, cols], z_bytes[:, cols], z[:, cols, :].rearrange("p v t -> p (v t)"))
            nc.tensor.matmul_mx(
                out=acc[h][:],
                lhsT=w4_codes[:].bitcast(FP8X4),
                lhsT_scale=w4_bytes[:],
                rhs=z_codes[:, cols].bitcast(FP8X4),
                rhs_scale=z_bytes[:, cols],
                start=True,
                stop=True,
            )
        for h, cols in enumerate(halves):
            result = keep.tile([N, HALF], F32, name=f"result_{h}")
            nc.vector.tensor_scalar_max(out=result[:], in0=acc[h][:], scalar1=0.0)
            nc.sync.dma_start(out=out[:, cols], in_=result[:])
